import numpy as np
CORES = [49,52,55,57,60,63,65,68,71,73,76,79]
N = 12
F = 256
B1, B2, LR, EPS = 0.75, 0.875, 2.0, 0.001
def setup_inputs(rng):
    idle = rng.random((128, N * F)) < 0.125; ib = np.stack([idle[:, F * r:F * r + F] for r in range(N)])
    return {"gr": (rng.standard_normal((N, 128, N * F), dtype=np.float32) * ~idle), "m": (rng.standard_normal((N, 128, F), dtype=np.float32) * np.where(ib, 0.004, 1.0)).astype(np.float32), "v": np.where(ib, 2e-6 * 50 ** rng.random((N, 128, F)), (0.5 + rng.standard_normal((N, 128, F), dtype=np.float32) ** 2) * N).astype(np.float32), "w": rng.standard_normal((N, 128, F), dtype=np.float32)}
def setup_inputs_big(rng):
    d = setup_inputs(rng)
    for k in ("gr", "m", "v", "w"): d[k] = (d[k].astype(np.float32) * 1024.0).astype(d[k].dtype)
    return d
def setup_inputs_small(rng):
    d = setup_inputs(rng)
    for k in ("gr", "m", "v", "w"): d[k] = (d[k].astype(np.float32) * (1 / 1024.0)).astype(d[k].dtype)
    return d
def setup_inputs_apart(rng):
    d = setup_inputs(rng)
    f = (10.0 ** rng.permutation(np.linspace(-1.5, 1.5, N))).astype(np.float32).reshape(N, 1, 1)
    for k in ("gr", "m", "v", "w"): d[k] = (d[k].astype(np.float32) * f).astype(d[k].dtype)
    return d
def reference(gr, m, v, w):
    GR, M, V, W = gr.astype(np.float64), m.astype(np.float64), v.astype(np.float64), w.astype(np.float64)
    s = GR.sum(axis=0)
    sb = np.stack([s[:, F * r:F * r + F] for r in range(N)])
    m2 = B1 * M + (1 - B1) * sb
    v2 = B2 * V + (1 - B2) * sb ** 2
    w2 = W - LR * m2 / (np.sqrt(v2) + EPS)
    return {"y": np.broadcast_to(np.concatenate(list(w2), axis=1).astype(np.float32), (N, 128, N * F)), "mo": m2.astype(np.float32), "vo": v2.astype(np.float32)}

import math
from concourse.bass import DstId, RemoteDMATransfer
from concourse.mybir import AluOpType, ActivationFunctionType

F = 256
W = 192
NCOL = 12 * F

SCRATCH = {
    "grb": ("sbuf", [128, NCOL], "float32"),
    "yb": ("sbuf", [128, NCOL], "float32"),
    "pack": ("sbuf", [128, 3 * F], "float32"),
    "mvl": ("sbuf", [128, 4 * W], "float32"),
    "raw": ("sbuf", [128, 12 * W], "float32"),
    "xl": ("sbuf", [128, 4 * W], "float32"),
    "vmw": ("sbuf", [128, 3 * W], "float32"),
    "agl": ("sbuf", [128, 5 * W], "float32"),
    "sR": ("sbuf", [128, W], "float32"),
    "sS": ("sbuf", [128, W], "float32"),
    "zz": ("sbuf", [128, W], "float32"),
    "rr": ("sbuf", [128, W], "float32"),
    "dd": ("sbuf", [128, W], "float32"),
    "qq": ("sbuf", [128, W], "float32"),
    "tt": ("sbuf", [128, W], "float32"),
    "mvo": ("sbuf", [128, 2 * W], "float32"),
    "wo": ("sbuf", [128, W], "float32"),
    "pA": ("psum", [128, 512], "float32"),
    "pB": ("psum", [128, 512], "float32"),
    "pSq": ("psum", [128, 512], "float32"),
    "pS3": ("psum", [128, 512], "float32"),
    "pU": ("psum", [128, 512], "float32"),
    "pW": ("psum", [128, 512], "float32"),
}
SEMAPHORES = (["ld%d" % i for i in range(4)] + ["ldv", "ldw", "go1", "go2", "go3", "sent"]
              + ["raw%d" % i for i in range(4)] + ["x%d" % i for i in range(4)] + ["va", "vb"]
              + ["ag%d" % i for i in range(4)] + ["y%d" % i for i in range(4)] + ["mvr", "sty", "stm"]
              + ["c%d" % i for i in range(1, 12)] + ["a%d" % i for i in range(1, 7)])


def _bits(mask):
    return [b for b in range(mask.bit_length()) if (mask >> b) & 1]


def _mask(bl):
    m = 0
    for b in bl:
        m |= 1 << b
    return m


def _stride(n):
    s = 1
    while s < n:
        s *= 2
    return s


def rank_program(g, core, T, topo):
    cores = list(T.cores)
    X = topo.chip(core)
    chips = sorted(set(topo.chip(c) for c in cores))
    if X not in chips:
        return
    every = range(topo.CHIPS * topo.CORES_PER_CHIP)
    ranks_on = {Y: [c for c in cores if topo.chip(c) == Y] for Y in chips}
    ports_on = {Y: [c for c in every if topo.chip(c) == Y and all(topo.may_write(c, d) for d in cores if d != c)]
                for Y in chips}
    helpers_on = {Y: [p for p in ports_on[Y] if p not in cores] for Y in chips}
    is_rank = core in cores
    is_port = core in ports_on[X]
    if not (is_rank or is_port):
        return
    S, V, A, Q = T.sem, g.vector, g.scalar, g.sync
    add, mult = AluOpType.add, AluOpType.mult
    Act = ActivationFunctionType

    def ci(Y):
        return chips.index(Y)

    def seg0(Y):
        return F * T.rank_of(ranks_on[Y][0])

    def far(Y):
        return sorted([Z for Z in chips if Z != Y],
                      key=lambda Z: 2 if topo.same_plane(Y, Z) else (1 if topo.mates(Y, Z) else 0))

    def quarter_pieces(Y, k):
        out = []
        for ri, r in enumerate(ranks_on[Y]):
            lo, hi = max(k * W, ri * F), min(k * W + W, ri * F + F)
            if lo < hi:
                out.append((r, lo - ri * F, hi - ri * F, lo - k * W))
        return out

    def rank_pieces(Y, r):
        return [(k, lo, hi, off) for k in range(len(ports_on[Y]))
                for (rr, lo, hi, off) in quarter_pieces(Y, k) if rr == r]

    def vmw_calls(Y, r):
        first, rest = [], []
        for (k, lo, hi, off) in rank_pieces(Y, r):
            p = ports_on[Y][k]
            if p == r:
                continue
            for u in range(3 * (hi - lo) // W):
                (first if u == 0 else rest).append((p, 3 * lo + u * W, 3 * off + u * W))
        return first, rest

    sent = [0]

    def tr(srcs, dsts, sem, eng, alu=0):
        sent[0] += len(eng)
        ids = [DstId(rid=topo.addr(d)[0], pnc=topo.addr(d)[1]) for d, _ in dsts]
        return RemoteDMATransfer(dst_ids=ids, dma_engine_mask=_mask(eng), remote_sem=sem, srcs=list(srcs),
                                 dsts=[ap for _, ap in dsts], alu_op=alu)

    def call(trs):
        g.remote_dma_fused(trs, local_sem=S.sent)

    def common_bits(dsts):
        m = topo.mask(core, dsts[0])
        for d in dsts[1:]:
            m &= topo.mask(core, d)
        return _bits(m)

    fo = far(X)
    steps = fo + [X]
    ports = ports_on[X]
    ranks = ranks_on[X]
    k = ports.index(core) if is_port else None
    others = [r for r in ranks if r != core]

    if is_rank:
        ri = ranks.index(core)
        for j, Y in enumerate(steps):
            if j == 3:
                Q.wait_ge(S.go1, 1)
            Q.dma_start(T.grb[:, seg0(Y):seg0(Y) + 3 * F], T.gr[:, seg0(Y):seg0(Y) + 3 * F]).then_inc(S["ld%d" % j], 16)
        mine = rank_pieces(X, core)
        early, late = [], []
        for (kk, lo, hi, _o) in mine:
            w = hi - lo
            for which, src in enumerate((T.v, T.m, T.w)):
                urgent = which == 0 or (ports[kk] != core and which * w < W)
                (early if urgent else late).append((T.pack[:, 3 * lo + which * w:3 * lo + (which + 1) * w],
                                                    src[:, lo:hi]))
        A.wait_ge(S.go2, 1)
        for dst, src in early:
            A.dma_start(dst, src).then_inc(S.ldv, 16)
        A.wait_ge(S.go3, 1)
        for dst, src in late:
            A.dma_start(dst, src).then_inc(S.ldw, 16)
        n_ldv, n_ldw = 16 * len(early), 16 * len(late)
        same = [p for p in ports if p != core and topo.die(p) == topo.die(core)]
        cross = [p for p in ports if p != core and topo.die(p) != topo.die(core)]
        slot = {}
        for i, p in enumerate(same):
            slot[p] = 2 * i
        for i, p in enumerate(cross):
            slot[p] = 2 * i + 1

    n_raw = 4 * len(others)

    def piece_src(Y, r):
        if r == core:
            return T.grb[:, seg0(Y) + k * W:seg0(Y) + k * W + W]
        s = ci(Y) * 3 + ranks.index(r)
        return T.raw[:, s * W:s * W + W]

    for j, Y in enumerate(steps):
        if is_rank:
            g.wait_ge(S["ld%d" % j], 16)
            trs = []
            for kk, p in enumerate(ports):
                if p == core:
                    continue
                s = ci(Y) * 3 + ri
                trs.append(tr([T.grb[:, seg0(Y) + kk * W:seg0(Y) + kk * W + W]], [(p, T.raw[:, s * W:s * W + W])],
                              S["raw%d" % ci(Y)], _bits(topo.mask(core, p))[slot[p]::4]))
            call(trs)
            if j >= 1:
                g.sem_inc(S["go%d" % j], 1)
        if is_port and j >= 1:
            Z = fo[j - 1]
            g.wait_ge(S["raw%d" % ci(Z)], n_raw)
            d = ports_on[Z][k]
            call([tr([piece_src(Z, r) for r in ranks], [(d, T.xl[:, ci(X) * W:ci(X) * W + W])], S["x%d" % ci(X)],
                     _bits(topo.mask(core, d)), alu=1)])

    if is_rank:
        first, rest = vmw_calls(X, core)
        for lst, sem, ldsem, n_ld in ((first, S.va, S.ldv, n_ldv), (rest, S.vb, S.ldw, n_ldw)):
            g.wait_ge(ldsem, n_ld)
            if lst:
                st = _stride(len(lst))
                call([tr([T.pack[:, a:a + W]], [(p, T.vmw[:, b:b + W])], sem, _bits(topo.mask(core, p))[i::st])
                      for i, (p, a, b) in enumerate(lst)])

    if is_port:
        n_va = n_vb = 0
        for r in others:
            first, rest = vmw_calls(X, r)
            n_va += sum(16 // _stride(len(first)) for (p, _a, _b) in first if p == core)
            n_vb += sum(16 // _stride(len(rest)) for (p, _a, _b) in rest if p == core)
        pcs = quarter_pieces(X, k)
        own_piece = any(r == core for (r, _l, _h, _o) in pcs)

        def part(r, lo, hi, off, which):
            w = hi - lo
            if r == core:
                return T.pack[:, 3 * lo + which * w:3 * lo + (which + 1) * w]
            return T.vmw[:, 3 * off + which * w:3 * off + (which + 1) * w]

        def wait_vmw(q, all_of_it):
            if n_va:
                q.wait_ge(S.va, n_va)
            if own_piece:
                q.wait_ge(S.ldv, n_ldv)
            if all_of_it:
                if n_vb:
                    q.wait_ge(S.vb, n_vb)
                if own_piece:
                    q.wait_ge(S.ldw, n_ldw)

        def xs(Y):
            return T.xl[:, ci(Y) * W:ci(Y) * W + W]

        wout = T.yb[:, seg0(X) + k * W:seg0(X) + k * W + W] if is_rank else T.wo[:, :]
        pA, pB, pSq, pS3, pU, pW = (T.pA[:, 0:W], T.pB[:, 0:W], T.pSq[:, 0:W], T.pS3[:, 0:W], T.pU[:, 0:W],
                                    T.pW[:, 0:W])
        V.wait_ge(S["x%d" % ci(fo[0])], 8)
        V.wait_ge(S["x%d" % ci(fo[1])], 8)
        V.tensor_tensor(pA, xs(fo[0]), xs(fo[1]), add).then_inc(S.c1, 1)
        V.wait_ge(S["raw%d" % ci(X)], n_raw)
        if is_rank:
            V.wait_ge(S.ld3, 16)
        V.tensor_tensor(pB, piece_src(X, ranks[0]), piece_src(X, ranks[1]), add).then_inc(S.c2, 1)
        V.wait_ge(S.c2, 1)
        V.tensor_tensor(T.sR[:, :], pB, piece_src(X, ranks[2]), add).then_inc(S.c3, 1)
        V.wait_ge(S.c1, 1)
        V.wait_ge(S.c3, 1)
        V.tensor_tensor(pA, pA, T.sR[:, :], add).then_inc(S.c4, 1)
        V.wait_ge(S.c4, 1)
        V.wait_ge(S["x%d" % ci(fo[2])], 8)
        V.tensor_tensor(T.sS[:, :], pA, xs(fo[2]), add).then_inc(S.c5, 1)
        A.wait_ge(S.c5, 1)
        A.activation(pSq, T.sS[:, :], Act.Square, scale=math.sqrt(1.0 / 7.0)).then_inc(S.a1, 1)
        A.activation(pS3, T.sS[:, :], Act.Copy, scale=1.0 / 3.0).then_inc(S.a2, 1)
        V.wait_ge(S.a1, 1)
        wait_vmw(V, False)
        for (r, lo, hi, off) in pcs:
            V.tensor_tensor(T.zz[:, off:off + hi - lo], T.pSq[:, off:off + hi - lo], part(r, lo, hi, off, 0),
                            add).then_inc(S.c6, 1)
        V.wait_ge(S.a2, 1)
        wait_vmw(V, True)
        for (r, lo, hi, off) in pcs:
            V.tensor_tensor(T.pU[:, off:off + hi - lo], T.pS3[:, off:off + hi - lo], part(r, lo, hi, off, 1),
                            add).then_inc(S.c7, 1)
        A.wait_ge(S.c6, len(pcs))
        A.activation(T.rr[:, :], T.zz[:, :], Act.Sqrt, scale=0.875).then_inc(S.a3, 1)
        A.activation(T.mvo[:, W:2 * W], T.zz[:, :], Act.Copy, scale=0.875).then_inc(S.a4, 1)
        A.wait_ge(S.c7, len(pcs))
        A.activation(T.mvo[:, 0:W], pU, Act.Copy, scale=0.75).then_inc(S.a5, 1)
        wait_vmw(A, True)
        for (r, lo, hi, off) in pcs:
            A.activation(T.pW[:, off:off + hi - lo], part(r, lo, hi, off, 2), Act.Copy).then_inc(S.a6, 1)
        V.wait_ge(S.a3, 1)
        V.tensor_scalar(T.dd[:, :], T.rr[:, :], -2.0 / 3.0, -0.002 / 3.0, mult, add).then_inc(S.c8, 1)
        V.wait_ge(S.c8, 1)
        V.reciprocal(T.qq[:, :], T.dd[:, :]).then_inc(S.c9, 1)
        V.wait_ge(S.c9, 1)
        V.wait_ge(S.c7, len(pcs))
        V.wait_ge(S.a5, 1)
        V.tensor_tensor(T.tt[:, :], pU, T.qq[:, :], mult).then_inc(S.c10, 1)
        V.wait_ge(S.c10, 1)
        V.wait_ge(S.a6, len(pcs))
        V.tensor_tensor(wout, pW, T.tt[:, :], add).then_inc(S.c11, 1)

        back = []
        for (r, _l, _h, _o) in pcs:
            if r != core:
                sl = [kk for (kk, _a, _b, _c) in rank_pieces(X, r)].index(k)
                back.append((r, T.mvl[:, sl * 2 * W:(sl + 1) * 2 * W]))
        g.wait_ge(S.a4, 1)
        g.wait_ge(S.a5, 1)
        if back:
            call([tr([T.mvo[:, :]], back, S.mvr, common_bits([r for r, _ in back]))])

        g.wait_ge(S.c11, 1)
        out = []
        for j, Y in enumerate(fo):
            if is_rank:
                out.append((helpers_on[Y][j], T.agl[:, 4 * W:5 * W]))
            else:
                out.append((ports_on[Y][k], T.agl[:, ci(X) * W:ci(X) * W + W]))
        off_eng = common_bits([d for d, _ in out])
        on_eng = [b for b in common_bits(others) if b not in off_eng]
        col = seg0(X) + k * W
        call([tr([wout], out, S["ag%d" % ci(X)], off_eng),
              tr([wout], [(r, T.yb[:, col:col + W]) for r in others], S["y%d" % ci(X)], on_eng)])

        if not is_rank:
            hi_ = helpers_on[X].index(core)
            for j, Y in enumerate(fo):
                todo = [(T.agl[:, ci(Y) * W:ci(Y) * W + W], seg0(Y) + k * W)]
                if j == hi_:
                    for kq, p in enumerate(ports_on[Y]):
                        if p in cores:
                            todo.append((T.agl[:, 4 * W:5 * W], seg0(Y) + kq * W))
                g.wait_ge(S["ag%d" % ci(Y)], 8 * len(todo))
                eng = common_bits(ranks)
                st = _stride(len(todo))
                call([tr([src], [(r, T.yb[:, c0:c0 + W]) for r in ranks], S["y%d" % ci(Y)], eng[i::st])
                      for i, (src, c0) in enumerate(todo)])

    if is_rank:
        n_on = len(_bits(topo.mask(core, others[0]))) - len(_bits(topo.mask(core, ranks_on[fo[0]][0])))
        Q.wait_ge(S["y%d" % ci(X)], n_on * len([p for p in ports if p != core]))
        if is_port:
            Q.wait_ge(S.c11, 1)
        Q.dma_start(T.y[:, seg0(X):seg0(X) + 3 * F], T.yb[:, seg0(X):seg0(X) + 3 * F]).then_inc(S.sty, 16)
        for Y in fo:
            Q.wait_ge(S["y%d" % ci(Y)], 16 * len(helpers_on[X]))
            Q.dma_start(T.y[:, seg0(Y):seg0(Y) + 3 * F], T.yb[:, seg0(Y):seg0(Y) + 3 * F]).then_inc(S.sty, 16)
        Q.wait_ge(S.sty, 16 * len(chips))

        n_back = 16 * len([1 for (kk, _a, _b, _c) in mine if ports[kk] != core])
        if n_back:
            A.wait_ge(S.mvr, n_back)
        if is_port:
            A.wait_ge(S.a4, 1)
            A.wait_ge(S.a5, 1)
        for sl, (kk, lo, hi, off) in enumerate(mine):
            buf, base = (T.mvo, 0) if ports[kk] == core else (T.mvl, sl * 2 * W)
            A.dma_start(T.mo[:, lo:hi], buf[:, base + off:base + off + hi - lo]).then_inc(S.stm, 16)
            A.dma_start(T.vo[:, lo:hi], buf[:, base + W + off:base + W + off + hi - lo]).then_inc(S.stm, 16)
        A.wait_ge(S.stm, 32 * len(mine))

    g.wait_ge(S.sent, sent[0])
